import numpy as np
import ml_dtypes


def mxq(x, axis, fmt="e4m3"):
    dtype, down = {"e4m3": (ml_dtypes.float8_e4m3fn, 7), "e5m2": (ml_dtypes.float8_e5m2, 14)}[fmt]
    v = np.moveaxis(np.asarray(x, np.float32).astype(ml_dtypes.bfloat16).astype(np.float64), axis, -1)
    blocks = v.reshape(v.shape[:-1] + (-1, 32))
    amax = np.abs(blocks).max(-1, keepdims=True)
    byte = np.maximum(np.where(amax > 0, np.frexp(amax)[1] - 1 + 127, 0) - down, 1)
    scale = np.exp2(byte - 127.0)
    codes = (blocks / scale).astype(np.float32).astype(dtype).astype(np.float64)
    return np.moveaxis((codes * scale).reshape(v.shape), -1, axis)


WIDE = False


def mx_kscale(k):
    if not WIDE:
        return np.ones(k)
    levels = np.array([10, -10, 5, -5, 0])
    if k % 512:
        return np.exp2(np.random.permutation(np.resize(levels, k // 32))).repeat(32)
    a = np.empty((k // 512, 16))
    for p in range(k // 512):
        a[p, :8] = np.random.permutation(np.resize(levels, 8))
        for g in range(8):
            far = levels[np.abs(levels - a[p, g]) >= 10]
            a[p, g + 8] = far[np.random.randint(len(far))]
    return np.exp2(a.ravel()).repeat(32)


def f64(x):
    return np.asarray(x).astype(np.float64)


def striped(idx):
    return np.tile(idx.reshape(-1, 16).T, (8, 1)).astype(np.uint16)


def unstriped(offs):
    return offs[:16].T.reshape(-1).astype(np.int64)


E2M1 = np.array([0.0, 0.5, 1.0, 1.5, 2.0, 3.0, 4.0, 6.0, -0.0, -0.5, -1.0, -1.5, -2.0, -3.0, -4.0, -6.0])


def pack_weight(w, fmt):
    k, n = w.shape
    w = f64(np.asarray(w, np.float32).astype(ml_dtypes.bfloat16)).reshape(k // 32, 32, n)
    amax = np.abs(w).max(1)
    if fmt == "e4m3":
        byte = np.frexp(amax)[1] - 1 + 127 - 7
    else:
        mant, ex = np.frexp(amax / 6.0)
        byte = np.where(mant > 0.5, ex, ex - 1) + 127
    byte = np.clip(np.where(amax > 0, byte, 1), 1, 254)
    scaled = (w * np.exp2(127.0 - byte)[:, None, :]).reshape(k, n).astype(np.float32)
    by_word = np.ascontiguousarray(scaled.reshape(k // 512, 128, 4, n).transpose(0, 1, 3, 2))
    if fmt == "e4m3":
        words = by_word.astype(ml_dtypes.float8_e4m3fn).view(np.uint8)
    else:
        c = by_word.astype(ml_dtypes.float4_e2m1fn).view(np.uint8) & 0xF
        words = (c[..., 0::2] | (c[..., 1::2] << 4)).reshape(k // 512, 128, 2 * n)
    return np.ascontiguousarray(words), np.ascontiguousarray(byte.astype(np.uint8).reshape(k // 512, 16, n))


def unpack_weight(words, scales, fmt):
    g, _, n = scales.shape
    words = np.ascontiguousarray(words).reshape(g, 128, n, -1)
    if fmt == "e4m3":
        vals = words.view(ml_dtypes.float8_e4m3fn).astype(np.float64)
    else:
        nib = np.empty((g, 128, n, 4), np.uint8)
        nib[..., 0::2] = words & 0xF
        nib[..., 1::2] = words >> 4
        vals = E2M1[nib]
    vals = vals * np.repeat(np.exp2(scales.astype(np.float64) - 127.0), 8, axis=1)[..., None]
    return vals.transpose(0, 1, 3, 2).reshape(g * 512, n)


def gelu(v):
    return 0.5 * v * (1.0 + np.tanh(np.sqrt(2.0 / np.pi) * (v + 0.044715 * v**3)))


def twice(P):
    return np.random.permutation(np.repeat(np.arange(P), 2))


K, T, S, H, P = 1536, 4096, 1024, 1024, 512


def setup_inputs():
    n = np.random.standard_normal
    s = mx_kscale(K)[:, None]
    u = mx_kscale(H)[:, None]
    d = {}
    d["tab_words"], d["tab_scales"] = pack_weight(n((K, T)) * s, "e4m3")
    d["offs"] = striped(np.random.permutation(T)[:S])
    d["w1"] = (n((K, H)) / s * u.T / K ** 0.5).astype(np.float32)
    d["b1"] = (0.5 * n(H) * u[:, 0]).astype(np.float32)
    d["pos1"] = striped(np.random.permutation(S)[:P])
    d["pos2"] = striped(np.random.permutation(S)[:P])
    d["gv"] = (1.3 * np.exp(0.3 * n(H)) / u[:, 0]).astype(np.float32)
    d["w4_words"], d["w4_scales"] = pack_weight(2.0 * n((H, H)) / u / H ** 0.5, "e2m1")
    d["pos3"] = striped(twice(P))
    d["sc"] = (1.5 * np.exp(0.3 * n(H)) / u[:, 0]).astype(np.float32)
    return d


def reference(tab_words, tab_scales, offs, w1, b1, pos1, pos2, gv,
              w4_words, w4_scales, pos3, sc):
    v = unpack_weight(tab_words, tab_scales, "e4m3")[:, unstriped(offs)]
    h = (mxq(f64(w1), 0, "e4m3").T @ v) + f64(b1)[:, None]
    first = h[:, unstriped(pos1)]
    second = h[:, unstriped(pos2)]
    x = first * np.tanh(f64(gv)[:, None] * second)
    w4 = unpack_weight(w4_words, w4_scales, "e2m1")
    y = w4.T @ mxq(x, 0, "e4m3")
    up = y[:, unstriped(pos3)]
    e = up + f64(sc)[:, None] * h
    return 1.0 / (1.0 + np.exp(-e))

@@ -1,0 +1,359 @@
+from contextlib import ExitStack
+
+import concourse.mybir as mybir
+
+K, T, S, H, PAIRS = 1536, 4096, 1024, 1024, 512
+FLOPS = 2 * K * H * S + 2 * H * H * PAIRS
+
+F32 = mybir.dt.float32
+BF16 = mybir.dt.bfloat16
+I32 = mybir.dt.int32
+U32 = mybir.dt.uint32
+U16 = mybir.dt.uint16
+U8 = mybir.dt.uint8
+FP8X4 = mybir.dt.float8_e4m3fn_x4
+FP4X4 = mybir.dt.float4_e2m1fn_x4
+ACT = mybir.ActivationFunctionType
+ALU = mybir.AluOpType
+
+P = 128
+PACK = 4
+K_PASS = P * PACK
+PASSES1 = K // K_PASS
+GROUPS = H // K_PASS
+BANK = 512
+QUADS = 4
+QUAD = 32
+SPARE = 16
+HELD = 2
+TAB_PIECE = 1024
+
+
+def tile_list_vending_refill_urgency_kernel(
+    tc, tab_words, tab_scales, offs, w1, b1, pos1, pos2, gv, w4_words, w4_scales, pos3, sc, out
+):
+    nc = tc.nc
+    with ExitStack() as ctx:
+        keep = ctx.enter_context(tc.tile_pool(name="keep", bufs=1))
+        psum = ctx.enter_context(tc.psum_pool(name="psum", bufs=1))
+
+        offs_t = keep.tile([P, S // 16], U16, name="offs_t")
+        pos1_t = keep.tile([P, PAIRS // 16], U16, name="pos1_t")
+        pos2_t = keep.tile([P, PAIRS // 16], U16, name="pos2_t")
+        pos3_t = keep.tile([P, S // 16], U16, name="pos3_t")
+        vecs = {}
+        y_tiles = []
+        raw = {}
+        w1_bf = {}
+        w1_codes = {}
+        w1_sc = {}
+        acc = {}
+        acc2 = {}
+        h = {}
+        second = {}
+        gate = {}
+        scaled = {}
+        dealt = {}
+        w4_raw = keep.tile([P, GROUPS, H // 2], I32, name="w4_raw")
+        w4_codes = keep.tile([P, GROUPS, H], U16, name="w4_codes", align_bytes=64)
+        v_sc = keep.tile([P, S], U8, name="v_sc", align_bytes=64)
+        v_words = {}
+        x_codes = [keep.tile([P, PAIRS], U32, name="x_codes%d" % b, align_bytes=64) for b in range(GROUPS)]
+        x_sc = [keep.tile([P, PAIRS], U8, name="x_sc%d" % b, align_bytes=64) for b in range(GROUPS)]
+        out_rows = out.rearrange("(b p t) j -> b t p j", b=GROUPS, t=PACK)
+
+        def load_w1(pool, b, a, parts, pieces=None):
+            width = K_PASS // parts
+            raw.setdefault((b, a), [])
+            for s in pieces or range(parts):
+                tile = pool.tile([P, PACK, width], F32, name="raw%d%d%d" % (b, a, s), tag="raw%d%d%d" % (b, a, s))
+                c0 = K_PASS * b + width * s
+                rows = w1[K_PASS * a : K_PASS * (a + 1), c0 : c0 + width]
+                nc.sync.dma_start(out=tile[:], in_=rows.rearrange("(p j) c -> p j c", j=PACK))
+                raw[b, a].append(tile)
+
+        def round_w1(b, a, s, engine):
+            if (b, a) not in w1_bf:
+                w1_bf[b, a] = keep.tile([P, PACK, P, PACK], BF16, name="w1_bf", tag="w1_bf", bufs=3, align_bytes=64)
+            src = raw[b, a][s]
+            ms = src.shape[2] // PACK
+            dst = w1_bf[b, a][:, :, ms * s : ms * (s + 1), :].rearrange("p t m j -> p m j t")
+            src = src[:].rearrange("p j (m t) -> p m j t", t=PACK)
+            if engine == "scalar":
+                nc.scalar.copy(out=dst, in_=src)
+            else:
+                nc.vector.tensor_copy(out=dst, in_=src)
+
+        def quantise_w1(b, a, t0, t1):
+            if (b, a) not in w1_codes:
+                w1_codes[b, a] = keep.tile([P, K_PASS], U32, name="w1c%d%d" % (b, a), align_bytes=64)
+                w1_sc[b, a] = keep.tile([P, K_PASS], U8, name="w1s%d%d" % (b, a), align_bytes=64)
+            nc.vector.quantize_mx(
+                out=w1_codes[b, a][:, P * t0 : P * t1].bitcast(FP8X4),
+                scales=w1_sc[b, a][:, P * t0 : P * t1],
+                in_=w1_bf[b, a][:, t0:t1].rearrange("p t m j -> p (t m j)"),
+            )
+
+        def stage1(b, a, t):
+            for half in range(2):
+                if a == 0:
+                    n = 2 * t + half
+                    acc[b, t, half] = psum.tile([P, BANK], F32, name="bank%d" % n, tag="bank%d" % n)
+                cols = slice(BANK * half, BANK * (half + 1))
+                nc.tensor.matmul_mx(
+                    out=acc[b, t, half][:],
+                    lhsT=w1_codes[b, a][:, P * t : P * (t + 1)].bitcast(FP8X4),
+                    lhsT_scale=w1_sc[b, a][:, P * t : P * (t + 1)],
+                    rhs=v_words[a][:, cols].bitcast(FP8X4),
+                    rhs_scale=v_sc[4 * a :, cols],
+                    start=(a == 0),
+                    stop=(a == PASSES1 - 1),
+                )
+
+        def bias_out(b, t, vector=False):
+            h[b, t] = keep.tile([P, S], F32, name="h%d%d" % (b, t))
+            for half in range(2):
+                cols = slice(BANK * half, BANK * (half + 1))
+                bias = vecs["b1"][:, b, t : t + 1]
+                if vector:
+                    nc.vector.tensor_scalar_add(h[b, t][:, cols], acc[b, t, half][:], bias)
+                else:
+                    nc.scalar.activation(out=h[b, t][:, cols], in_=acc[b, t, half][:], func=ACT.Identity, bias=bias)
+
+        def deal_w4(g, copy):
+            cols = slice(K_PASS * g, K_PASS * (g + 1))
+            copy(
+                out=w4_codes[:, :, cols].rearrange("p a (t m) -> p a t m", t=PACK),
+                in_=w4_raw[:].bitcast(U16)[:, :, cols].rearrange("p a (m t) -> p a t m", t=PACK),
+            )
+
+        def stage2(i, a):
+            if a == 0:
+                acc2[i] = psum.tile([P, BANK], F32, name="bank%d" % i, tag="bank%d" % i)
+            nc.tensor.matmul_mx(
+                out=acc2[i][:],
+                lhsT=w4_codes[:, a, P * i : P * (i + 1)].bitcast(FP4X4),
+                lhsT_scale=dealt["w4_sc"][:, H * a + P * i : H * a + P * (i + 1)],
+                rhs=x_codes[a][:].bitcast(FP8X4),
+                rhs_scale=x_sc[a][:],
+                start=(a == 0),
+                stop=(a == GROUPS - 1),
+            )
+
+        def y_out(i):
+            nc.scalar.copy(out=y_tiles[i][:, :PAIRS], in_=acc2[i][:])
+
+        with tc.tile_pool(name="early", bufs=1) as early:
+            tab_sc = keep.tile([P, T], U8, name="tab_sc", tag="v1", align_bytes=64)
+            nc.vector.memset(tab_sc[:].bitcast(I32), 0)
+
+            def load_tab_scales():
+                for q in range(QUADS):
+                    nc.sync.dma_start(
+                        out=tab_sc[QUAD * q : QUAD * q + 4 * PASSES1, :].bitcast(I32),
+                        in_=tab_scales[:, 4 * q : 4 * q + 4, :].bitcast(I32),
+                    )
+
+            w4_sc_raw = early.tile([P, GROUPS * H], U8, name="w4_sc_raw", align_bytes=64)
+            nc.vector.memset(w4_sc_raw[:].bitcast(I32), 0)
+            for q in range(QUADS):
+                nc.gpsimd.dma_start(
+                    out=w4_sc_raw[QUAD * q : QUAD * q + 4, :].bitcast(I32).rearrange("r (a c) -> r a c", a=GROUPS),
+                    in_=w4_scales[:, 4 * q : 4 * q + 4, :].bitcast(I32).rearrange("a r c -> r a c"),
+                )
+
+            def load_vec(name, vec):
+                vecs[name] = keep.tile([P, GROUPS, PACK], F32, name=name + "_t")
+                nc.sync.dma_start(out=vecs[name][:], in_=vec.rearrange("(b p t) -> p b t", b=GROUPS, t=PACK))
+
+            for i in range(GROUPS * PACK):
+                y = keep.tile([P, PAIRS + SPARE], F32, name="y%d" % i)
+                nc.vector.memset(y[:, PAIRS:], 0.0)
+                y_tiles.append(y)
+
+            tab_t = {a: early.tile([P, T], I32, name="tab%d" % a) for a in (0, 2)}
+            tab_t[1] = keep.tile([P, T], I32, name="tab1", tag="tab1", align_bytes=64)
+
+            def deal_w4_scales():
+                dealt["w4_sc"] = keep.tile([P, GROUPS * H], U8, name="w4_sc", tag="tab1", align_bytes=64)
+                nc.vector.tensor_copy(
+                    out=dealt["w4_sc"][:].rearrange("p (g t m) -> p g t m", t=PACK, m=P),
+                    in_=w4_sc_raw[:].rearrange("p (g m t) -> p g t m", t=PACK, m=P),
+                )
+
+            def load_tab(a, first=0, last=T):
+                words = tab_words[a].rearrange("p t i -> p (t i)").bitcast(I32)
+                for c0 in range(first, last, TAB_PIECE):
+                    nc.sync.dma_start(out=tab_t[a][:, c0 : c0 + TAB_PIECE], in_=words[:, c0 : c0 + TAB_PIECE])
+
+            def gather_tab(a):
+                v_words[a] = keep.tile([P, S], U32, name="v%d" % a, tag="v%d" % a, align_bytes=64)
+                nc.vector.tensor_copy(out=v_words[a][:], in_=tab_t[a][:].bitcast(U32).indirect(offs_t[:]))
+
+            load_tab(0)
+            nc.sync.dma_start(offs_t[:], offs)
+            load_w1(early, 0, 0, 2)
+            load_tab(1, 0, TAB_PIECE)
+            load_tab_scales()
+            load_tab(1, TAB_PIECE, T)
+            load_w1(early, 0, 1, 1)
+            load_tab(2)
+            load_w1(early, 0, 2, 2)
+            load_vec("b1", b1)
+            nc.sync.dma_start(pos2_t[:], pos2)
+            load_w1(keep, 1, 0, 2, [0])
+            load_vec("gv", gv)
+            nc.sync.dma_start(pos1_t[:], pos1)
+            load_w1(keep, 1, 0, 2, [1])
+            load_w1(keep, 1, 1, 2)
+            load_w1(keep, 1, 2, 2)
+            load_vec("sc", sc)
+            nc.sync.dma_start(out=w4_raw[:], in_=w4_words.bitcast(I32).rearrange("a p c -> p a c"))
+            nc.sync.dma_start(pos3_t[:], pos3)
+            gather_tab(0)
+            nc.vector.tensor_copy(out=v_sc[:], in_=tab_sc[:].indirect(offs_t[:]))
+            for a in range(PASSES1 - 1):
+                for s in range(len(raw[0, a])):
+                    round_w1(0, a, s, "scalar")
+                quantise_w1(0, a, 0, PACK)
+                for t in range(PACK):
+                    stage1(0, a, t)
+                gather_tab(a + 1)
+                if a == 0:
+                    deal_w4_scales()
+            round_w1(0, 2, 0, "scalar")
+            round_w1(0, 2, 1, "vector")
+
+        late = ctx.enter_context(tc.tile_pool(name="late", bufs=1))
+        x32 = [late.tile([P, PACK, PAIRS], F32, name="x32_%d" % b, tag="x32_%d" % b, align_bytes=64) for b in range(GROUPS)]
+        x_bf = [late.tile([P, PAIRS, PACK], BF16, name="x_bf%d" % b, tag="x_bf%d" % b, align_bytes=64) for b in range(GROUPS)]
+
+        def pick_second(b, t):
+            second[b, t] = late.tile([P, PAIRS], F32, name="second", tag="second", bufs=3)
+            nc.vector.tensor_copy(out=second[b, t][:], in_=h[b, t][:].indirect(pos2_t[:]))
+
+        def tanh_gate(b, t):
+            if (b, t) == (GROUPS - 1, PACK - 1):
+                gate[b, t] = late.tile([P, PAIRS], F32, name="gate_last", tag="held")
+            else:
+                gate[b, t] = late.tile([P, PAIRS], F32, name="gate", tag="gate", bufs=3)
+            nc.scalar.activation(out=gate[b, t][:], in_=second[b, t][:], func=ACT.Tanh, scale=vecs["gv"][:, b, t : t + 1])
+
+        def pick_first(b, t):
+            nc.vector.tensor_tensor(x32[b][:, t, :], h[b, t][:].indirect(pos1_t[:]), gate[b, t][:], ALU.mult)
+
+        def round_x(b, m0, m1, engine):
+            dst = x_bf[b][:, m0:m1, :].rearrange("p (c i) t -> p c t i", i=4)
+            src = x32[b][:, :, m0:m1].rearrange("p t (c i) -> p c t i", i=4)
+            if engine == "scalar":
+                nc.scalar.copy(out=dst, in_=src)
+            else:
+                nc.vector.tensor_copy(out=dst, in_=src)
+
+        def quantise_x(b):
+            nc.vector.quantize_mx(
+                out=x_codes[b][:].bitcast(FP8X4), scales=x_sc[b][:], in_=x_bf[b][:].rearrange("p m t -> p (m t)")
+            )
+
+        def scale_h(i, engine, tag):
+            b, t = divmod(i, PACK)
+            if tag == "held":
+                if "held" not in scaled:
+                    scaled["held"] = late.tile([P, HELD, S], F32, name="held", tag="held")
+                    scaled["count"] = 0
+                scaled[i] = scaled["held"][:, scaled["count"], :]
+                scaled["count"] = scaled["count"] + 1
+            else:
+                pool = keep if tag.startswith("raw") else late
+                scaled[i] = pool.tile([P, S], F32, name="scaled%d" % i, tag=tag, align_bytes=64)[:]
+            factor = vecs["sc"][:, b, t : t + 1]
+            if engine == "scalar":
+                nc.scalar.activation(out=scaled[i], in_=h[b, t][:], func=ACT.Copy, scale=factor)
+            else:
+                nc.vector.tensor_scalar_mul(scaled[i], h[b, t][:], factor)
+
+        def finish(i, half):
+            b, t = divmod(i, PACK)
+            cols = slice(BANK * half, BANK * (half + 1))
+            lists = pos3_t[:, BANK // 16 * half : BANK // 16 * (half + 1)]
+            e = late.tile([P, BANK], F32, name="e", tag="e", bufs=4)
+            nc.vector.tensor_tensor(e[:], y_tiles[i][:].indirect(lists), scaled[i][:, cols], ALU.add)
+            o = late.tile([P, BANK], F32, name="o", tag="o", bufs=6)
+            nc.scalar.activation(out=o[:], in_=e[:], func=ACT.Sigmoid)
+            nc.sync.dma_start(out=out_rows[b, t][:, cols], in_=o[:])
+
+        quantise_w1(0, 2, 0, 1)
+        stage1(0, 2, 0)
+        quantise_w1(0, 2, 1, PACK)
+        for t in range(1, PACK):
+            stage1(0, 2, t)
+        round_w1(1, 0, 0, "scalar")
+        bias_out(0, 0, vector=True)
+        bias_out(0, 1)
+        pick_second(0, 0)
+        tanh_gate(0, 0)
+        pick_second(0, 1)
+        bias_out(0, 2)
+        pick_first(0, 0)
+        tanh_gate(0, 1)
+        bias_out(0, 3)
+        pick_second(0, 2)
+        round_w1(1, 0, 1, "vector")
+        tanh_gate(0, 2)
+        round_w1(1, 1, 0, "scalar")
+        pick_first(0, 1)
+        quantise_w1(1, 0, 0, PACK)
+        for t in range(PACK):
+            stage1(1, 0, t)
+        round_w1(1, 1, 1, "scalar")
+        pick_second(0, 3)
+        tanh_gate(0, 3)
+        round_w1(1, 2, 0, "vector")
+        round_w1(1, 2, 1, "vector")
+        quantise_w1(1, 1, 0, PACK)
+        quantise_w1(1, 2, 0, PACK)
+        for t in range(PACK):
+            stage1(1, 1, t)
+            stage1(1, 2, t)
+        deal_w4(0, nc.scalar.copy)
+        deal_w4(1, nc.scalar.copy)
+        pick_first(0, 2)
+        pick_first(0, 3)
+        bias_out(1, 0)
+        bias_out(1, 1)
+        pick_second(1, 0)
+        tanh_gate(1, 0)
+        pick_second(1, 1)
+        bias_out(1, 2)
+        pick_first(1, 0)
+        tanh_gate(1, 1)
+        bias_out(1, 3)
+        pick_second(1, 2)
+        tanh_gate(1, 2)
+        round_x(0, 0, PAIRS // 2, "scalar")
+        pick_first(1, 1)
+        pick_second(1, 3)
+        round_x(0, PAIRS // 2, PAIRS, "scalar")
+        tanh_gate(1, 3)
+        pick_first(1, 2)
+        quantise_x(0)
+        for i in range(GROUPS * PACK):
+            stage2(i, 0)
+        scale_h(0, "scalar", "x32_0")
+        pick_first(1, 3)
+        round_x(1, 0, 192, "scalar")
+        round_x(1, 192, PAIRS, "vector")
+        scale_h(1, "vector", "held")
+        quantise_x(1)
+        for i in range(GROUPS * PACK):
+            stage2(i, 1)
+        scale_h(2, "vector", "held")
+        y_out(0)
+        y_out(1)
+        for i in range(GROUPS * PACK):
+            finish(i, 0)
+            if i + 2 < GROUPS * PACK:
+                y_out(i + 2)
+            finish(i, 1)
+            if i + 3 < GROUPS * PACK:
+                scale_h(i + 3, "scalar", ("x32_1", "x_bf1", "x32_0")[i % 3])

@@ -21,12 +21,13 @@ PACK = 4
 K_PASS = P * PACK
 PASSES1 = K // K_PASS
 GROUPS = H // K_PASS
+TILES = GROUPS * PACK
 BANK = 512
 QUADS = 4
 QUAD = 32
 SPARE = 16
-HELD = 2
 TAB_PIECE = 1024
+X_SCALAR = 176
 
 
 def tile_list_vending_refill_urgency_kernel(
@@ -37,61 +38,48 @@ def tile_list_vending_refill_urgency_kernel(
         keep = ctx.enter_context(tc.tile_pool(name="keep", bufs=1))
         psum = ctx.enter_context(tc.psum_pool(name="psum", bufs=1))
 
+        def tile(pool, shape, dtype, name, tag=None):
+            return pool.tile(shape, dtype, name=name, tag=tag or name, align_bytes=64)
+
         offs_t = keep.tile([P, S // 16], U16, name="offs_t")
         pos1_t = keep.tile([P, PAIRS // 16], U16, name="pos1_t")
         pos2_t = keep.tile([P, PAIRS // 16], U16, name="pos2_t")
         pos3_t = keep.tile([P, S // 16], U16, name="pos3_t")
-        vecs = {}
-        y_tiles = []
-        raw = {}
-        w1_bf = {}
-        w1_codes = {}
-        w1_sc = {}
-        acc = {}
-        acc2 = {}
-        h = {}
-        second = {}
-        gate = {}
-        scaled = {}
-        dealt = {}
-        w4_raw = keep.tile([P, GROUPS, H // 2], I32, name="w4_raw")
-        w4_codes = keep.tile([P, GROUPS, H], U16, name="w4_codes", align_bytes=64)
-        v_sc = keep.tile([P, S], U8, name="v_sc", align_bytes=64)
-        v_words = {}
-        x_codes = [keep.tile([P, PAIRS], U32, name="x_codes%d" % b, align_bytes=64) for b in range(GROUPS)]
-        x_sc = [keep.tile([P, PAIRS], U8, name="x_sc%d" % b, align_bytes=64) for b in range(GROUPS)]
+        vecs, raw, w1_bf, w1_codes, w1_sc, v_words = {}, {}, {}, {}, {}, {}
+        acc, acc2, h, second, gate, scaled, w4, x_bf = {}, {}, {}, {}, {}, {}, {}, {}
+        w4_raw = tile(keep, [P, GROUPS, H // 2], I32, "w4_raw")
+        v_sc = tile(keep, [P, S], U8, "v_sc")
+        x_codes = [tile(keep, [P, PAIRS], U32, "x_codes%d" % b) for b in range(GROUPS)]
+        x_sc = [tile(keep, [P, PAIRS], U8, "x_sc%d" % b) for b in range(GROUPS)]
+        y_tiles = [tile(keep, [P, PAIRS + SPARE], F32, "y%d" % i) for i in range(TILES)]
         out_rows = out.rearrange("(b p t) j -> b t p j", b=GROUPS, t=PACK)
 
-        def load_w1(pool, b, a, parts, pieces=None):
-            width = K_PASS // parts
-            raw.setdefault((b, a), [])
-            for s in pieces or range(parts):
-                tile = pool.tile([P, PACK, width], F32, name="raw%d%d%d" % (b, a, s), tag="raw%d%d%d" % (b, a, s))
-                c0 = K_PASS * b + width * s
-                rows = w1[K_PASS * a : K_PASS * (a + 1), c0 : c0 + width]
-                nc.sync.dma_start(out=tile[:], in_=rows.rearrange("(p j) c -> p j c", j=PACK))
-                raw[b, a].append(tile)
+        def load_vec(name, vec):
+            vecs[name] = tile(keep, [P, GROUPS, 2 * PACK], F32, name)
+            nc.sync.dma_start(out=vecs[name][:, :, :PACK], in_=vec.rearrange("(b p t) -> p b t", b=GROUPS, t=PACK))
 
-        def round_w1(b, a, s, engine):
-            if (b, a) not in w1_bf:
-                w1_bf[b, a] = keep.tile([P, PACK, P, PACK], BF16, name="w1_bf", tag="w1_bf", bufs=3, align_bytes=64)
-            src = raw[b, a][s]
-            ms = src.shape[2] // PACK
-            dst = w1_bf[b, a][:, :, ms * s : ms * (s + 1), :].rearrange("p t m j -> p m j t")
-            src = src[:].rearrange("p j (m t) -> p m j t", t=PACK)
-            if engine == "scalar":
-                nc.scalar.copy(out=dst, in_=src)
-            else:
-                nc.vector.tensor_copy(out=dst, in_=src)
+        def load_w1(pool, b, a):
+            raw[b, a] = tile(pool, [P, PACK, K_PASS], F32, "raw%d%d" % (b, a))
+            rows = w1[K_PASS * a : K_PASS * (a + 1), K_PASS * b : K_PASS * (b + 1)]
+            nc.sync.dma_start(out=raw[b, a][:], in_=rows.rearrange("(p j) c -> p j c", j=PACK))
 
-        def quantise_w1(b, a, t0, t1):
+        def round_w1(b, a, t0, t1, copy, pool, tag=None):
+            w1_bf[b, a, t0] = tile(pool, [P, t1 - t0, P, PACK], BF16, "w1_bf%d%d%d" % (b, a, t0), tag)
+            copy(
+                out=w1_bf[b, a, t0][:].rearrange("p t m j -> p m j t"),
+                in_=raw[b, a][:].rearrange("p j (m t) -> p m j t", t=PACK)[:, :, :, t0:t1],
+            )
+
+        def quantise_w1(b, a, t0):
             if (b, a) not in w1_codes:
-                w1_codes[b, a] = keep.tile([P, K_PASS], U32, name="w1c%d%d" % (b, a), align_bytes=64)
-                w1_sc[b, a] = keep.tile([P, K_PASS], U8, name="w1s%d%d" % (b, a), align_bytes=64)
+                w1_codes[b, a] = tile(keep, [P, K_PASS], U32, "w1_codes%d%d" % (b, a))
+                w1_sc[b, a] = tile(keep, [P, K_PASS], U8, "w1_sc%d%d" % (b, a))
+            src = w1_bf[b, a, t0]
+            cols = slice(P * t0, P * (t0 + src.shape[1]))
             nc.vector.quantize_mx(
-                out=w1_codes[b, a][:, P * t0 : P * t1].bitcast(FP8X4),
-                scales=w1_sc[b, a][:, P * t0 : P * t1],
-                in_=w1_bf[b, a][:, t0:t1].rearrange("p t m j -> p (t m j)"),
+                out=w1_codes[b, a][:, cols].bitcast(FP8X4),
+                scales=w1_sc[b, a][:, cols],
+                in_=src[:].rearrange("p t m j -> p (t m j)"),
             )
 
         def stage1(b, a, t):
@@ -111,7 +99,7 @@ def tile_list_vending_refill_urgency_kernel(
                 )
 
         def bias_out(b, t, vector=False):
-            h[b, t] = keep.tile([P, S], F32, name="h%d%d" % (b, t))
+            h[b, t] = tile(keep, [P, S], F32, "h%d%d" % (b, t))
             for half in range(2):
                 cols = slice(BANK * half, BANK * (half + 1))
                 bias = vecs["b1"][:, b, t : t + 1]
@@ -120,20 +108,13 @@ def tile_list_vending_refill_urgency_kernel(
                 else:
                     nc.scalar.activation(out=h[b, t][:, cols], in_=acc[b, t, half][:], func=ACT.Identity, bias=bias)
 
-        def deal_w4(g, copy):
-            cols = slice(K_PASS * g, K_PASS * (g + 1))
-            copy(
-                out=w4_codes[:, :, cols].rearrange("p a (t m) -> p a t m", t=PACK),
-                in_=w4_raw[:].bitcast(U16)[:, :, cols].rearrange("p a (m t) -> p a t m", t=PACK),
-            )
-
         def stage2(i, a):
             if a == 0:
                 acc2[i] = psum.tile([P, BANK], F32, name="bank%d" % i, tag="bank%d" % i)
             nc.tensor.matmul_mx(
                 out=acc2[i][:],
-                lhsT=w4_codes[:, a, P * i : P * (i + 1)].bitcast(FP4X4),
-                lhsT_scale=dealt["w4_sc"][:, H * a + P * i : H * a + P * (i + 1)],
+                lhsT=w4["codes"][:, a, P * i : P * (i + 1)].bitcast(FP4X4),
+                lhsT_scale=w4["scales"][:, H * a + P * i : H * a + P * (i + 1)],
                 rhs=x_codes[a][:].bitcast(FP8X4),
                 rhs_scale=x_sc[a][:],
                 start=(a == 0),
@@ -144,179 +125,170 @@ def tile_list_vending_refill_urgency_kernel(
             nc.scalar.copy(out=y_tiles[i][:, :PAIRS], in_=acc2[i][:])
 
         with tc.tile_pool(name="early", bufs=1) as early:
-            tab_sc = keep.tile([P, T], U8, name="tab_sc", tag="v1", align_bytes=64)
+            tab_sc = tile(early, [P, T], U8, "tab_sc")
+            w4_sc_raw = tile(early, [P, GROUPS * H], U8, "w4_sc_raw")
+            tab_t = [tile(keep if a == 1 else early, [P, T], I32, "tab%d" % a) for a in range(PASSES1)]
             nc.vector.memset(tab_sc[:].bitcast(I32), 0)
+            nc.vector.memset(w4_sc_raw[:].bitcast(I32), 0)
+            for y in y_tiles:
+                nc.vector.memset(y[:, PAIRS:], 0.0)
 
             def load_tab_scales():
                 for q in range(QUADS):
-                    nc.sync.dma_start(
+                    nc.gpsimd.dma_start(
                         out=tab_sc[QUAD * q : QUAD * q + 4 * PASSES1, :].bitcast(I32),
                         in_=tab_scales[:, 4 * q : 4 * q + 4, :].bitcast(I32),
                     )
 
-            w4_sc_raw = early.tile([P, GROUPS * H], U8, name="w4_sc_raw", align_bytes=64)
-            nc.vector.memset(w4_sc_raw[:].bitcast(I32), 0)
-            for q in range(QUADS):
-                nc.gpsimd.dma_start(
-                    out=w4_sc_raw[QUAD * q : QUAD * q + 4, :].bitcast(I32).rearrange("r (a c) -> r a c", a=GROUPS),
-                    in_=w4_scales[:, 4 * q : 4 * q + 4, :].bitcast(I32).rearrange("a r c -> r a c"),
-                )
-
-            def load_vec(name, vec):
-                vecs[name] = keep.tile([P, GROUPS, PACK], F32, name=name + "_t")
-                nc.sync.dma_start(out=vecs[name][:], in_=vec.rearrange("(b p t) -> p b t", b=GROUPS, t=PACK))
-
-            for i in range(GROUPS * PACK):
-                y = keep.tile([P, PAIRS + SPARE], F32, name="y%d" % i)
-                nc.vector.memset(y[:, PAIRS:], 0.0)
-                y_tiles.append(y)
-
-            tab_t = {a: early.tile([P, T], I32, name="tab%d" % a) for a in (0, 2)}
-            tab_t[1] = keep.tile([P, T], I32, name="tab1", tag="tab1", align_bytes=64)
-
-            def deal_w4_scales():
-                dealt["w4_sc"] = keep.tile([P, GROUPS * H], U8, name="w4_sc", tag="tab1", align_bytes=64)
-                nc.vector.tensor_copy(
-                    out=dealt["w4_sc"][:].rearrange("p (g t m) -> p g t m", t=PACK, m=P),
-                    in_=w4_sc_raw[:].rearrange("p (g m t) -> p g t m", t=PACK, m=P),
-                )
+            def load_w4_scales():
+                for q in range(QUADS):
+                    nc.gpsimd.dma_start(
+                        out=w4_sc_raw[QUAD * q : QUAD * q + 4, :].bitcast(I32).rearrange("r (a c) -> r a c", a=GROUPS),
+                        in_=w4_scales[:, 4 * q : 4 * q + 4, :].bitcast(I32).rearrange("a r c -> r a c"),
+                    )
 
             def load_tab(a, first=0, last=T):
                 words = tab_words[a].rearrange("p t i -> p (t i)").bitcast(I32)
                 for c0 in range(first, last, TAB_PIECE):
                     nc.sync.dma_start(out=tab_t[a][:, c0 : c0 + TAB_PIECE], in_=words[:, c0 : c0 + TAB_PIECE])
 
-            def gather_tab(a):
-                v_words[a] = keep.tile([P, S], U32, name="v%d" % a, tag="v%d" % a, align_bytes=64)
+            def gather_tab(a, tag=None):
+                v_words[a] = tile(keep, [P, S], U32, "v%d" % a, tag)
                 nc.vector.tensor_copy(out=v_words[a][:], in_=tab_t[a][:].bitcast(U32).indirect(offs_t[:]))
 
+            def deal_w4_scales():
+                w4["scales"] = tile(keep, [P, GROUPS * H], U8, "w4_sc", "tab1")
+                nc.vector.tensor_copy(
+                    out=w4["scales"][:].rearrange("p (g t m) -> p g t m", t=PACK, m=P),
+                    in_=w4_sc_raw[:].rearrange("p (g m t) -> p g t m", t=PACK, m=P),
+                )
+
+            load_tab_scales()
+            load_w4_scales()
             load_tab(0)
             nc.sync.dma_start(offs_t[:], offs)
-            load_w1(early, 0, 0, 2)
-            load_tab(1, 0, TAB_PIECE)
-            load_tab_scales()
-            load_tab(1, TAB_PIECE, T)
-            load_w1(early, 0, 1, 1)
+            load_w1(early, 0, 0)
+            load_tab(1, 0, 2 * TAB_PIECE)
+
+            load_tab(1, 2 * TAB_PIECE, T)
+            load_w1(early, 0, 1)
             load_tab(2)
-            load_w1(early, 0, 2, 2)
+            load_w1(early, 0, 2)
             load_vec("b1", b1)
             nc.sync.dma_start(pos2_t[:], pos2)
-            load_w1(keep, 1, 0, 2, [0])
+            load_w1(keep, 1, 0)
             load_vec("gv", gv)
             nc.sync.dma_start(pos1_t[:], pos1)
-            load_w1(keep, 1, 0, 2, [1])
-            load_w1(keep, 1, 1, 2)
-            load_w1(keep, 1, 2, 2)
+            load_w1(keep, 1, 1)
+            load_w1(keep, 1, 2)
             load_vec("sc", sc)
             nc.sync.dma_start(out=w4_raw[:], in_=w4_words.bitcast(I32).rearrange("a p c -> p a c"))
             nc.sync.dma_start(pos3_t[:], pos3)
             gather_tab(0)
             nc.vector.tensor_copy(out=v_sc[:], in_=tab_sc[:].indirect(offs_t[:]))
             for a in range(PASSES1 - 1):
-                for s in range(len(raw[0, a])):
-                    round_w1(0, a, s, "scalar")
-                quantise_w1(0, a, 0, PACK)
+                round_w1(0, a, 0, PACK, nc.scalar.copy, keep, "v%d" % (a + 1))
+                quantise_w1(0, a, 0)
                 for t in range(PACK):
                     stage1(0, a, t)
                 gather_tab(a + 1)
                 if a == 0:
                     deal_w4_scales()
-            round_w1(0, 2, 0, "scalar")
-            round_w1(0, 2, 1, "vector")
+            round_w1(0, 2, 0, 2, nc.vector.tensor_copy, keep)
+            round_w1(0, 2, 2, 4, nc.scalar.copy, keep)
 
         late = ctx.enter_context(tc.tile_pool(name="late", bufs=1))
-        x32 = [late.tile([P, PACK, PAIRS], F32, name="x32_%d" % b, tag="x32_%d" % b, align_bytes=64) for b in range(GROUPS)]
-        x_bf = [late.tile([P, PAIRS, PACK], BF16, name="x_bf%d" % b, tag="x_bf%d" % b, align_bytes=64) for b in range(GROUPS)]
+        x32 = [tile(late, [P, PACK, PAIRS], F32, "x32_%d" % b) for b in range(GROUPS)]
 
         def pick_second(b, t):
-            second[b, t] = late.tile([P, PAIRS], F32, name="second", tag="second", bufs=3)
+            second[b, t] = tile(late, [P, PAIRS], F32, "second%d%d" % (b, t))
             nc.vector.tensor_copy(out=second[b, t][:], in_=h[b, t][:].indirect(pos2_t[:]))
 
         def tanh_gate(b, t):
-            if (b, t) == (GROUPS - 1, PACK - 1):
-                gate[b, t] = late.tile([P, PAIRS], F32, name="gate_last", tag="held")
-            else:
-                gate[b, t] = late.tile([P, PAIRS], F32, name="gate", tag="gate", bufs=3)
+            gate[b, t] = tile(late, [P, PAIRS], F32, "gate%d%d" % (b, t))
             nc.scalar.activation(out=gate[b, t][:], in_=second[b, t][:], func=ACT.Tanh, scale=vecs["gv"][:, b, t : t + 1])
 
         def pick_first(b, t):
             nc.vector.tensor_tensor(x32[b][:, t, :], h[b, t][:].indirect(pos1_t[:]), gate[b, t][:], ALU.mult)
 
-        def round_x(b, m0, m1, engine):
-            dst = x_bf[b][:, m0:m1, :].rearrange("p (c i) t -> p c t i", i=4)
-            src = x32[b][:, :, m0:m1].rearrange("p t (c i) -> p c t i", i=4)
-            if engine == "scalar":
-                nc.scalar.copy(out=dst, in_=src)
-            else:
-                nc.vector.tensor_copy(out=dst, in_=src)
+        def deal_w4(g):
+            if g == 0:
+                w4["codes"] = tile(late, [P, GROUPS, H], U16, "w4_codes", "second02")
+            cols = slice(K_PASS * g, K_PASS * (g + 1))
+            nc.scalar.copy(
+                out=w4["codes"][:, :, cols].rearrange("p a (t m) -> p a t m", t=PACK),
+                in_=w4_raw[:].bitcast(U16)[:, :, cols].rearrange("p a (m t) -> p a t m", t=PACK),
+            )
+
+        def round_x(b, m0, m1, copy, tag=None):
+            if b not in x_bf:
+                x_bf[b] = tile(late, [P, PAIRS, PACK], BF16, "x_bf%d" % b, tag)
+            copy(
+                out=x_bf[b][:, m0:m1, :].rearrange("p (c i) t -> p c t i", i=4),
+                in_=x32[b][:, :, m0:m1].rearrange("p t (c i) -> p c t i", i=4),
+            )
 
         def quantise_x(b):
             nc.vector.quantize_mx(
                 out=x_codes[b][:].bitcast(FP8X4), scales=x_sc[b][:], in_=x_bf[b][:].rearrange("p m t -> p (m t)")
             )
 
-        def scale_h(i, engine, tag):
+        def scale_h(i, vector, tag):
             b, t = divmod(i, PACK)
-            if tag == "held":
-                if "held" not in scaled:
-                    scaled["held"] = late.tile([P, HELD, S], F32, name="held", tag="held")
-                    scaled["count"] = 0
-                scaled[i] = scaled["held"][:, scaled["count"], :]
-                scaled["count"] = scaled["count"] + 1
-            else:
-                pool = keep if tag.startswith("raw") else late
-                scaled[i] = pool.tile([P, S], F32, name="scaled%d" % i, tag=tag, align_bytes=64)[:]
+            scaled[i] = tile(late, [P, S], F32, "scaled%d" % i, tag)
             factor = vecs["sc"][:, b, t : t + 1]
-            if engine == "scalar":
-                nc.scalar.activation(out=scaled[i], in_=h[b, t][:], func=ACT.Copy, scale=factor)
+            if vector:
+                nc.vector.tensor_scalar_mul(scaled[i][:], h[b, t][:], factor)
             else:
-                nc.vector.tensor_scalar_mul(scaled[i], h[b, t][:], factor)
+                nc.scalar.activation(out=scaled[i][:], in_=h[b, t][:], func=ACT.Copy, scale=factor)
 
-        def finish(i, half):
+        def finish(i, j0, j1):
             b, t = divmod(i, PACK)
-            cols = slice(BANK * half, BANK * (half + 1))
-            lists = pos3_t[:, BANK // 16 * half : BANK // 16 * (half + 1)]
-            e = late.tile([P, BANK], F32, name="e", tag="e", bufs=4)
-            nc.vector.tensor_tensor(e[:], y_tiles[i][:].indirect(lists), scaled[i][:, cols], ALU.add)
-            o = late.tile([P, BANK], F32, name="o", tag="o", bufs=6)
+            e = late.tile([P, j1 - j0], F32, name="e", tag="e", bufs=4)
+            window = y_tiles[i][:].indirect(pos3_t[:, j0 // 16 : j1 // 16])
+            nc.vector.tensor_tensor(e[:], window, scaled[i][:, j0:j1], ALU.add)
+            o = late.tile([P, j1 - j0], F32, name="o", tag="o", bufs=6)
             nc.scalar.activation(out=o[:], in_=e[:], func=ACT.Sigmoid)
-            nc.sync.dma_start(out=out_rows[b, t][:, cols], in_=o[:])
+            nc.sync.dma_start(out=out_rows[b, t][:, j0:j1], in_=o[:])
 
-        quantise_w1(0, 2, 0, 1)
+        quantise_w1(0, 2, 0)
         stage1(0, 2, 0)
-        quantise_w1(0, 2, 1, PACK)
-        for t in range(1, PACK):
-            stage1(0, 2, t)
-        round_w1(1, 0, 0, "scalar")
+        stage1(0, 2, 1)
+        quantise_w1(0, 2, 2)
+        stage1(0, 2, 2)
+        stage1(0, 2, 3)
+        round_w1(1, 0, 0, 2, nc.scalar.copy, late)
         bias_out(0, 0, vector=True)
         bias_out(0, 1)
         pick_second(0, 0)
         tanh_gate(0, 0)
+        round_w1(1, 0, 2, 4, nc.vector.tensor_copy, keep, "w1_codes02")
+        quantise_w1(1, 0, 0)
+        quantise_w1(1, 0, 2)
         pick_second(0, 1)
-        bias_out(0, 2)
+        round_w1(1, 1, 0, 2, nc.scalar.copy, late, "second00")
         pick_first(0, 0)
+        bias_out(0, 2)
         tanh_gate(0, 1)
-        bias_out(0, 3)
+        round_w1(1, 2, 0, 2, nc.vector.tensor_copy, late, "gate00")
+        round_w1(1, 1, 2, 4, nc.scalar.copy, late, "second01")
         pick_second(0, 2)
-        round_w1(1, 0, 1, "vector")
-        tanh_gate(0, 2)
-        round_w1(1, 1, 0, "scalar")
         pick_first(0, 1)
-        quantise_w1(1, 0, 0, PACK)
+        bias_out(0, 3)
         for t in range(PACK):
             stage1(1, 0, t)
-        round_w1(1, 1, 1, "scalar")
-        pick_second(0, 3)
-        tanh_gate(0, 3)
-        round_w1(1, 2, 0, "vector")
-        round_w1(1, 2, 1, "vector")
-        quantise_w1(1, 1, 0, PACK)
-        quantise_w1(1, 2, 0, PACK)
+        tanh_gate(0, 2)
+        round_w1(1, 2, 2, 4, nc.vector.tensor_copy, late, "gate01")
+        for t0 in (0, 2):
+            quantise_w1(1, 1, t0)
+            quantise_w1(1, 2, t0)
         for t in range(PACK):
             stage1(1, 1, t)
             stage1(1, 2, t)
-        deal_w4(0, nc.scalar.copy)
-        deal_w4(1, nc.scalar.copy)
+        deal_w4(0)
+        deal_w4(1)
+        pick_second(0, 3)
+        tanh_gate(0, 3)
         pick_first(0, 2)
         pick_first(0, 3)
         bias_out(1, 0)
@@ -330,30 +302,35 @@ def tile_list_vending_refill_urgency_kernel(
         bias_out(1, 3)
         pick_second(1, 2)
         tanh_gate(1, 2)
-        round_x(0, 0, PAIRS // 2, "scalar")
+        round_x(0, 0, PAIRS // 2, nc.scalar.copy, "second11")
         pick_first(1, 1)
         pick_second(1, 3)
-        round_x(0, PAIRS // 2, PAIRS, "scalar")
+        round_x(0, PAIRS // 2, PAIRS, nc.scalar.copy)
         tanh_gate(1, 3)
         pick_first(1, 2)
         quantise_x(0)
-        for i in range(GROUPS * PACK):
+        for i in range(TILES):
             stage2(i, 0)
-        scale_h(0, "scalar", "x32_0")
+        scale_h(0, False, "x32_0")
         pick_first(1, 3)
-        round_x(1, 0, 192, "scalar")
-        round_x(1, 192, PAIRS, "vector")
-        scale_h(1, "vector", "held")
+        round_x(1, 0, X_SCALAR, nc.scalar.copy)
+        round_x(1, X_SCALAR, PAIRS, nc.vector.tensor_copy)
         quantise_x(1)
-        for i in range(GROUPS * PACK):
+        for i in range(TILES):
             stage2(i, 1)
-        scale_h(2, "vector", "held")
+        scale_h(1, True, "x_bf1")
+        scale_h(2, True, "gate13")
         y_out(0)
         y_out(1)
-        for i in range(GROUPS * PACK):
-            finish(i, 0)
-            if i + 2 < GROUPS * PACK:
+        last = TILES - 1
+        for i in range(last):
+            finish(i, 0, BANK)
+            if i + 2 <= last:
                 y_out(i + 2)
-            finish(i, 1)
-            if i + 3 < GROUPS * PACK:
-                scale_h(i + 3, "scalar", ("x32_1", "x_bf1", "x32_0")[i % 3])
+            finish(i, BANK, S)
+            if i + 3 <= last:
+                scale_h(i + 3, False, ("x32_1", "x32_0", "x_bf1", "gate13", "x32_1")[i])
+        finish(last, 0, 512)
+        finish(last, 512, 768)
+        finish(last, 768, 896)
+        finish(last, 896, S)

@@ -65,10 +65,11 @@ def tile_list_vending_refill_urgency_kernel(
 
         def round_w1(b, a, t0, t1, copy, pool, tag=None):
             w1_bf[b, a, t0] = tile(pool, [P, t1 - t0, P, PACK], BF16, "w1_bf%d%d%d" % (b, a, t0), tag)
-            copy(
-                out=w1_bf[b, a, t0][:].rearrange("p t m j -> p m j t"),
-                in_=raw[b, a][:].rearrange("p j (m t) -> p m j t", t=PACK)[:, :, :, t0:t1],
-            )
+            for u in range(t0, t1, 2):
+                copy(
+                    out=w1_bf[b, a, t0][:, u - t0 : u - t0 + 2].rearrange("p t m j -> p m j t"),
+                    in_=raw[b, a][:].rearrange("p j (m t) -> p m j t", t=PACK)[:, :, :, u : u + 2],
+                )
 
         def quantise_w1(b, a, t0):
             if (b, a) not in w1_codes:

from contextlib import ExitStack

import concourse.mybir as mybir

K, T, S, H, PAIRS = 1536, 4096, 1024, 1024, 512
FLOPS = 2 * K * H * S + 2 * H * H * PAIRS

F32 = mybir.dt.float32
BF16 = mybir.dt.bfloat16
I32 = mybir.dt.int32
U32 = mybir.dt.uint32
U16 = mybir.dt.uint16
U8 = mybir.dt.uint8
FP8X4 = mybir.dt.float8_e4m3fn_x4
FP4X4 = mybir.dt.float4_e2m1fn_x4
ACT = mybir.ActivationFunctionType
ALU = mybir.AluOpType

P = 128
PACK = 4
K_PASS = P * PACK
PASSES1 = K // K_PASS
GROUPS = H // K_PASS
TILES = GROUPS * PACK
BANK = 512
QUADS = 4
QUAD = 32
SPARE = 16
TAB_PIECE = 1024
X_SCALAR = 176


def tile_list_vending_refill_urgency_kernel(
    tc, tab_words, tab_scales, offs, w1, b1, pos1, pos2, gv, w4_words, w4_scales, pos3, sc, out
):
    nc = tc.nc
    with ExitStack() as ctx:
        keep = ctx.enter_context(tc.tile_pool(name="keep", bufs=1))
        psum = ctx.enter_context(tc.psum_pool(name="psum", bufs=1))

        def tile(pool, shape, dtype, name, tag=None):
            return pool.tile(shape, dtype, name=name, tag=tag or name, align_bytes=64)

        offs_t = keep.tile([P, S // 16], U16, name="offs_t")
        pos1_t = keep.tile([P, PAIRS // 16], U16, name="pos1_t")
        pos2_t = keep.tile([P, PAIRS // 16], U16, name="pos2_t")
        pos3_t = keep.tile([P, S // 16], U16, name="pos3_t")
        vecs, raw, w1_bf, w1_codes, w1_sc, v_words = {}, {}, {}, {}, {}, {}
        acc, acc2, h, second, gate, scaled, w4, x_bf = {}, {}, {}, {}, {}, {}, {}, {}
        w4_raw = tile(keep, [P, GROUPS, H // 2], I32, "w4_raw")
        v_sc = tile(keep, [P, S], U8, "v_sc")
        x_codes = [tile(keep, [P, PAIRS], U32, "x_codes%d" % b) for b in range(GROUPS)]
        x_sc = [tile(keep, [P, PAIRS], U8, "x_sc%d" % b) for b in range(GROUPS)]
        y_tiles = [tile(keep, [P, PAIRS + SPARE], F32, "y%d" % i) for i in range(TILES)]
        out_rows = out.rearrange("(b p t) j -> b t p j", b=GROUPS, t=PACK)

        def load_vec(name, vec):
            vecs[name] = tile(keep, [P, GROUPS, 2 * PACK], F32, name)
            nc.sync.dma_start(out=vecs[name][:, :, :PACK], in_=vec.rearrange("(b p t) -> p b t", b=GROUPS, t=PACK))

        def load_w1(pool, b, a):
            raw[b, a] = tile(pool, [P, PACK, K_PASS], F32, "raw%d%d" % (b, a))
            rows = w1[K_PASS * a : K_PASS * (a + 1), K_PASS * b : K_PASS * (b + 1)]
            nc.sync.dma_start(out=raw[b, a][:], in_=rows.rearrange("(p j) c -> p j c", j=PACK))

        def round_w1(b, a, t0, t1, copy, pool, tag=None):
            w1_bf[b, a, t0] = tile(pool, [P, t1 - t0, P, PACK], BF16, "w1_bf%d%d%d" % (b, a, t0), tag)
            for u in range(t0, t1, 2):
                copy(
                    out=w1_bf[b, a, t0][:, u - t0 : u - t0 + 2].rearrange("p t m j -> p m j t"),
                    in_=raw[b, a][:].rearrange("p j (m t) -> p m j t", t=PACK)[:, :, :, u : u + 2],
                )

        def quantise_w1(b, a, t0):
            if (b, a) not in w1_codes:
                w1_codes[b, a] = tile(keep, [P, K_PASS], U32, "w1_codes%d%d" % (b, a))
                w1_sc[b, a] = tile(keep, [P, K_PASS], U8, "w1_sc%d%d" % (b, a))
            src = w1_bf[b, a, t0]
            cols = slice(P * t0, P * (t0 + src.shape[1]))
            nc.vector.quantize_mx(
                out=w1_codes[b, a][:, cols].bitcast(FP8X4),
                scales=w1_sc[b, a][:, cols],
                in_=src[:].rearrange("p t m j -> p (t m j)"),
            )

        def stage1(b, a, t):
            for half in range(2):
                if a == 0:
                    n = 2 * t + half
                    acc[b, t, half] = psum.tile([P, BANK], F32, name="bank%d" % n, tag="bank%d" % n)
                cols = slice(BANK * half, BANK * (half + 1))
                nc.tensor.matmul_mx(
                    out=acc[b, t, half][:],
                    lhsT=w1_codes[b, a][:, P * t : P * (t + 1)].bitcast(FP8X4),
                    lhsT_scale=w1_sc[b, a][:, P * t : P * (t + 1)],
                    rhs=v_words[a][:, cols].bitcast(FP8X4),
                    rhs_scale=v_sc[4 * a :, cols],
                    start=(a == 0),
                    stop=(a == PASSES1 - 1),
                )

        def bias_out(b, t, vector=False):
            h[b, t] = tile(keep, [P, S], F32, "h%d%d" % (b, t))
            for half in range(2):
                cols = slice(BANK * half, BANK * (half + 1))
                bias = vecs["b1"][:, b, t : t + 1]
                if vector:
                    nc.vector.tensor_scalar_add(h[b, t][:, cols], acc[b, t, half][:], bias)
                else:
                    nc.scalar.activation(out=h[b, t][:, cols], in_=acc[b, t, half][:], func=ACT.Identity, bias=bias)

        def stage2(i, a):
            if a == 0:
                acc2[i] = psum.tile([P, BANK], F32, name="bank%d" % i, tag="bank%d" % i)
            nc.tensor.matmul_mx(
                out=acc2[i][:],
                lhsT=w4["codes"][:, a, P * i : P * (i + 1)].bitcast(FP4X4),
                lhsT_scale=w4["scales"][:, H * a + P * i : H * a + P * (i + 1)],
                rhs=x_codes[a][:].bitcast(FP8X4),
                rhs_scale=x_sc[a][:],
                start=(a == 0),
                stop=(a == GROUPS - 1),
            )

        def y_out(i):
            nc.scalar.copy(out=y_tiles[i][:, :PAIRS], in_=acc2[i][:])

        with tc.tile_pool(name="early", bufs=1) as early:
            tab_sc = tile(early, [P, T], U8, "tab_sc")
            w4_sc_raw = tile(early, [P, GROUPS * H], U8, "w4_sc_raw")
            tab_t = [tile(keep if a == 1 else early, [P, T], I32, "tab%d" % a) for a in range(PASSES1)]
            nc.vector.memset(tab_sc[:].bitcast(I32), 0)
            nc.vector.memset(w4_sc_raw[:].bitcast(I32), 0)
            for y in y_tiles:
                nc.vector.memset(y[:, PAIRS:], 0.0)

            def load_tab_scales():
                for q in range(QUADS):
                    nc.gpsimd.dma_start(
                        out=tab_sc[QUAD * q : QUAD * q + 4 * PASSES1, :].bitcast(I32),
                        in_=tab_scales[:, 4 * q : 4 * q + 4, :].bitcast(I32),
                    )

            def load_w4_scales():
                for q in range(QUADS):
                    nc.gpsimd.dma_start(
                        out=w4_sc_raw[QUAD * q : QUAD * q + 4, :].bitcast(I32).rearrange("r (a c) -> r a c", a=GROUPS),
                        in_=w4_scales[:, 4 * q : 4 * q + 4, :].bitcast(I32).rearrange("a r c -> r a c"),
                    )

            def load_tab(a, first=0, last=T):
                words = tab_words[a].rearrange("p t i -> p (t i)").bitcast(I32)
                for c0 in range(first, last, TAB_PIECE):
                    nc.sync.dma_start(out=tab_t[a][:, c0 : c0 + TAB_PIECE], in_=words[:, c0 : c0 + TAB_PIECE])

            def gather_tab(a, tag=None):
                v_words[a] = tile(keep, [P, S], U32, "v%d" % a, tag)
                nc.vector.tensor_copy(out=v_words[a][:], in_=tab_t[a][:].bitcast(U32).indirect(offs_t[:]))

            def deal_w4_scales():
                w4["scales"] = tile(keep, [P, GROUPS * H], U8, "w4_sc", "tab1")
                nc.vector.tensor_copy(
                    out=w4["scales"][:].rearrange("p (g t m) -> p g t m", t=PACK, m=P),
                    in_=w4_sc_raw[:].rearrange("p (g m t) -> p g t m", t=PACK, m=P),
                )

            load_tab_scales()
            load_w4_scales()
            load_tab(0)
            nc.sync.dma_start(offs_t[:], offs)
            load_w1(early, 0, 0)
            load_tab(1, 0, 2 * TAB_PIECE)

            load_tab(1, 2 * TAB_PIECE, T)
            load_w1(early, 0, 1)
            load_tab(2)
            load_w1(early, 0, 2)
            load_vec("b1", b1)
            nc.sync.dma_start(pos2_t[:], pos2)
            load_w1(keep, 1, 0)
            load_vec("gv", gv)
            nc.sync.dma_start(pos1_t[:], pos1)
            load_w1(keep, 1, 1)
            load_w1(keep, 1, 2)
            load_vec("sc", sc)
            nc.sync.dma_start(out=w4_raw[:], in_=w4_words.bitcast(I32).rearrange("a p c -> p a c"))
            nc.sync.dma_start(pos3_t[:], pos3)
            gather_tab(0)
            nc.vector.tensor_copy(out=v_sc[:], in_=tab_sc[:].indirect(offs_t[:]))
            for a in range(PASSES1 - 1):
                round_w1(0, a, 0, PACK, nc.scalar.copy, keep, "v%d" % (a + 1))
                quantise_w1(0, a, 0)
                for t in range(PACK):
                    stage1(0, a, t)
                gather_tab(a + 1)
                if a == 0:
                    deal_w4_scales()
            round_w1(0, 2, 0, 2, nc.vector.tensor_copy, keep)
            round_w1(0, 2, 2, 4, nc.scalar.copy, keep)

        late = ctx.enter_context(tc.tile_pool(name="late", bufs=1))
        x32 = [tile(late, [P, PACK, PAIRS], F32, "x32_%d" % b) for b in range(GROUPS)]

        def pick_second(b, t):
            second[b, t] = tile(late, [P, PAIRS], F32, "second%d%d" % (b, t))
            nc.vector.tensor_copy(out=second[b, t][:], in_=h[b, t][:].indirect(pos2_t[:]))

        def tanh_gate(b, t):
            gate[b, t] = tile(late, [P, PAIRS], F32, "gate%d%d" % (b, t))
            nc.scalar.activation(out=gate[b, t][:], in_=second[b, t][:], func=ACT.Tanh, scale=vecs["gv"][:, b, t : t + 1])

        def pick_first(b, t):
            nc.vector.tensor_tensor(x32[b][:, t, :], h[b, t][:].indirect(pos1_t[:]), gate[b, t][:], ALU.mult)

        def deal_w4(g):
            if g == 0:
                w4["codes"] = tile(late, [P, GROUPS, H], U16, "w4_codes", "second02")
            cols = slice(K_PASS * g, K_PASS * (g + 1))
            nc.scalar.copy(
                out=w4["codes"][:, :, cols].rearrange("p a (t m) -> p a t m", t=PACK),
                in_=w4_raw[:].bitcast(U16)[:, :, cols].rearrange("p a (m t) -> p a t m", t=PACK),
            )

        def round_x(b, m0, m1, copy, tag=None):
            if b not in x_bf:
                x_bf[b] = tile(late, [P, PAIRS, PACK], BF16, "x_bf%d" % b, tag)
            copy(
                out=x_bf[b][:, m0:m1, :].rearrange("p (c i) t -> p c t i", i=4),
                in_=x32[b][:, :, m0:m1].rearrange("p t (c i) -> p c t i", i=4),
            )

        def quantise_x(b):
            nc.vector.quantize_mx(
                out=x_codes[b][:].bitcast(FP8X4), scales=x_sc[b][:], in_=x_bf[b][:].rearrange("p m t -> p (m t)")
            )

        def scale_h(i, vector, tag):
            b, t = divmod(i, PACK)
            scaled[i] = tile(late, [P, S], F32, "scaled%d" % i, tag)
            factor = vecs["sc"][:, b, t : t + 1]
            if vector:
                nc.vector.tensor_scalar_mul(scaled[i][:], h[b, t][:], factor)
            else:
                nc.scalar.activation(out=scaled[i][:], in_=h[b, t][:], func=ACT.Copy, scale=factor)

        def finish(i, j0, j1):
            b, t = divmod(i, PACK)
            e = late.tile([P, j1 - j0], F32, name="e", tag="e", bufs=4)
            window = y_tiles[i][:].indirect(pos3_t[:, j0 // 16 : j1 // 16])
            nc.vector.tensor_tensor(e[:], window, scaled[i][:, j0:j1], ALU.add)
            o = late.tile([P, j1 - j0], F32, name="o", tag="o", bufs=6)
            nc.scalar.activation(out=o[:], in_=e[:], func=ACT.Sigmoid)
            nc.sync.dma_start(out=out_rows[b, t][:, j0:j1], in_=o[:])

        quantise_w1(0, 2, 0)
        stage1(0, 2, 0)
        stage1(0, 2, 1)
        quantise_w1(0, 2, 2)
        stage1(0, 2, 2)
        stage1(0, 2, 3)
        round_w1(1, 0, 0, 2, nc.scalar.copy, late)
        bias_out(0, 0, vector=True)
        bias_out(0, 1)
        pick_second(0, 0)
        tanh_gate(0, 0)
        round_w1(1, 0, 2, 4, nc.vector.tensor_copy, keep, "w1_codes02")
        quantise_w1(1, 0, 0)
        quantise_w1(1, 0, 2)
        pick_second(0, 1)
        round_w1(1, 1, 0, 2, nc.scalar.copy, late, "second00")
        pick_first(0, 0)
        bias_out(0, 2)
        tanh_gate(0, 1)
        round_w1(1, 2, 0, 2, nc.vector.tensor_copy, late, "gate00")
        round_w1(1, 1, 2, 4, nc.scalar.copy, late, "second01")
        pick_second(0, 2)
        pick_first(0, 1)
        bias_out(0, 3)
        for t in range(PACK):
            stage1(1, 0, t)
        tanh_gate(0, 2)
        round_w1(1, 2, 2, 4, nc.vector.tensor_copy, late, "gate01")
        for t0 in (0, 2):
            quantise_w1(1, 1, t0)
            quantise_w1(1, 2, t0)
        for t in range(PACK):
            stage1(1, 1, t)
            stage1(1, 2, t)
        deal_w4(0)
        deal_w4(1)
        pick_second(0, 3)
        tanh_gate(0, 3)
        pick_first(0, 2)
        pick_first(0, 3)
        bias_out(1, 0)
        bias_out(1, 1)
        pick_second(1, 0)
        tanh_gate(1, 0)
        pick_second(1, 1)
        bias_out(1, 2)
        pick_first(1, 0)
        tanh_gate(1, 1)
        bias_out(1, 3)
        pick_second(1, 2)
        tanh_gate(1, 2)
        round_x(0, 0, PAIRS // 2, nc.scalar.copy, "second11")
        pick_first(1, 1)
        pick_second(1, 3)
        round_x(0, PAIRS // 2, PAIRS, nc.scalar.copy)
        tanh_gate(1, 3)
        pick_first(1, 2)
        quantise_x(0)
        for i in range(TILES):
            stage2(i, 0)
        scale_h(0, False, "x32_0")
        pick_first(1, 3)
        round_x(1, 0, X_SCALAR, nc.scalar.copy)
        round_x(1, X_SCALAR, PAIRS, nc.vector.tensor_copy)
        quantise_x(1)
        for i in range(TILES):
            stage2(i, 1)
        scale_h(1, True, "x_bf1")
        scale_h(2, True, "gate13")
        y_out(0)
        y_out(1)
        last = TILES - 1
        for i in range(last):
            finish(i, 0, BANK)
            if i + 2 <= last:
                y_out(i + 2)
            finish(i, BANK, S)
            if i + 3 <= last:
                scale_h(i + 3, False, ("x32_1", "x32_0", "x_bf1", "gate13", "x32_1")[i])
        finish(last, 0, 512)
        finish(last, 512, 768)
        finish(last, 768, 896)
        finish(last, 896, S)
